import numpy as np
import ml_dtypes


def mxq(x, axis, fmt="e4m3"):
    dtype, down = {"e4m3": (ml_dtypes.float8_e4m3fn, 7), "e5m2": (ml_dtypes.float8_e5m2, 14)}[fmt]
    v = np.moveaxis(np.asarray(x, np.float32).astype(ml_dtypes.bfloat16).astype(np.float64), axis, -1)
    blocks = v.reshape(v.shape[:-1] + (-1, 32))
    amax = np.abs(blocks).max(-1, keepdims=True)
    byte = np.maximum(np.where(amax > 0, np.frexp(amax)[1] - 1 + 127, 0) - down, 1)
    scale = np.exp2(byte - 127.0)
    codes = (blocks / scale).astype(np.float32).astype(dtype).astype(np.float64)
    return np.moveaxis((codes * scale).reshape(v.shape), -1, axis)


WIDE = False


def mx_kscale(k):
    if not WIDE:
        return np.ones(k)
    levels = np.array([10, -10, 5, -5, 0])
    if k % 512:
        return np.exp2(np.random.permutation(np.resize(levels, k // 32))).repeat(32)
    a = np.empty((k // 512, 16))
    for p in range(k // 512):
        a[p, :8] = np.random.permutation(np.resize(levels, 8))
        for g in range(8):
            far = levels[np.abs(levels - a[p, g]) >= 10]
            a[p, g + 8] = far[np.random.randint(len(far))]
    return np.exp2(a.ravel()).repeat(32)


def f64(x):
    return np.asarray(x).astype(np.float64)


def striped(idx):
    return np.tile(idx.reshape(-1, 16).T, (8, 1)).astype(np.uint16)


def unstriped(offs):
    return offs[:16].T.reshape(-1).astype(np.int64)


def pack_weight(w):
    k, n = w.shape
    w = f64(np.asarray(w, np.float32).astype(ml_dtypes.bfloat16)).reshape(k // 32, 32, n)
    amax = np.abs(w).max(1)
    byte = np.clip(np.where(amax > 0, np.frexp(amax)[1] - 1 + 127 - 7, 1), 1, 254)
    scaled = (w * np.exp2(127.0 - byte)[:, None, :]).reshape(k, n).astype(np.float32)
    words = np.ascontiguousarray(scaled.reshape(k // 512, 128, 4, n).transpose(0, 1, 3, 2)).astype(ml_dtypes.float8_e4m3fn).view(np.uint8)
    return words, np.ascontiguousarray(byte.astype(np.uint8).reshape(k // 512, 16, n))


def unpack_weight(words, scales):
    g, p, n, _ = words.shape
    vals = np.ascontiguousarray(words).view(ml_dtypes.float8_e4m3fn).astype(np.float64) * np.repeat(np.exp2(scales.astype(np.float64) - 127.0), 8, axis=1)[..., None]
    return vals.transpose(0, 1, 3, 2).reshape(g * 512, n)


K, T, S, N = 1024, 4096, 1024, 128
P = 2 ** 7


def setup_inputs():
    n = np.random.standard_normal
    s = mx_kscale(K)[:, None]
    packed_xT = pack_weight(n((K, T)) * s)
    return {
        "x_words": packed_xT[0],
        "x_scales": packed_xT[1],
        "w1": (n((K, N)) / np.sqrt(K) / s).astype(np.float32),
        "truth": (np.random.uniform(0.3, 3.0, (N, S))).astype(np.float32),
        "valid": (np.tile(np.random.uniform(0.2, 1.0, S), (P, 1))).astype(np.float32),
        "offs": striped(np.random.permutation(T)[:S]),
    }


def reference(x_words, x_scales, w1, truth, valid, offs):
    xq = unpack_weight(x_words, x_scales)[:, unstriped(offs)]
    y = mxq(f64(w1), 0, "e4m3").T @ xq
    ld = y - (np.log(f64(truth)))
    ldm = ld.mean(axis=1, keepdims=True)
    return f64(valid)[:1] * np.abs(ld - ldm) + 0.5 * (np.abs(ld - (np.pad(ld, ((0, 0), (0, 1)))[:, 1:])))

@@ -1,0 +1,156 @@
+from contextlib import ExitStack
+
+import concourse.mybir as mybir
+
+K, T, S, M = 1024, 4096, 1024, 128
+FLOPS = 2 * K * S * M
+
+F32 = mybir.dt.float32
+BF16 = mybir.dt.bfloat16
+I32 = mybir.dt.int32
+U32 = mybir.dt.uint32
+U16 = mybir.dt.uint16
+U8 = mybir.dt.uint8
+FP8X4 = mybir.dt.float8_e4m3fn_x4
+ALU = mybir.AluOpType
+ACT = mybir.ActivationFunctionType
+
+P = 128
+PACK = 4
+PASSES = K // (P * PACK)
+HALF = S // 2
+GROUPS = ((0, 512), (512, 768), (768, 1024))
+CHUNK = 256
+CHUNKS = S // CHUNK
+
+
+def tile_picked_yslog_edge_p_kernel(tc, x_words, x_scales, w1, truth, valid, offs, out):
+    nc = tc.nc
+    with ExitStack() as ctx:
+        keep = ctx.enter_context(tc.tile_pool(name="keep", bufs=1))
+        psum = ctx.enter_context(tc.psum_pool(name="psum", bufs=1))
+
+        offsets = keep.tile([P, S // 16], U16, name="offsets")
+        nc.sync.dma_start(offsets[:], offs)
+
+        scale_table = keep.tile([P, T], U8, name="scale_table", tag="scales_then_codes", align_bytes=64)
+        nc.vector.memset(scale_table[:].bitcast(I32), 0)
+        scale_rows = x_scales.bitcast(I32)
+        for q in range(4):
+            nc.gpsimd.dma_start(
+                scale_table[:].bitcast(I32)[32 * q : 32 * q + 4 * PASSES, :], scale_rows[:, 4 * q : 4 * q + 4, :]
+            )
+
+        ld = keep.tile([P, S + 8], F32, name="ld")
+        one = keep.tile([P, 1], F32, name="one")
+        nc.vector.memset(one[:], 1.0)
+        nc.scalar.activation(ld[:, S : S + 1], one[:], ACT.Ln)
+
+        word_tables = [keep.tile([P, T], I32, name="word_table%d" % o, align_bytes=64) for o in range(PASSES)]
+        w_raw = [keep.tile([P, PACK, M], F32, name="w_raw%d" % o) for o in range(PASSES)]
+        truth_sb = [keep.tile([P, HALF], F32, name="truth%d" % h) for h in range(2)]
+        valid_sb = keep.tile([P, S], F32, name="valid_sb")
+
+        def load_words(o):
+            nc.sync.dma_start(word_tables[o][:], x_words[o].rearrange("p n t -> p (n t)").bitcast(I32))
+
+        load_words(0)
+        for o in range(PASSES):
+            nc.sync.dma_start(w_raw[o][:], w1[o * P * PACK : (o + 1) * P * PACK, :].rearrange("(p j) m -> p j m", j=PACK))
+        load_words(1)
+        for h in range(2):
+            nc.sync.dma_start(truth_sb[h][:], truth[:, h * HALF : (h + 1) * HALF])
+        nc.sync.dma_start(valid_sb[:], valid)
+
+        x_scale = keep.tile([P, S], U8, name="x_scale", align_bytes=64)
+        nc.vector.tensor_copy(x_scale[:], scale_table[:].indirect(offsets[:]))
+
+        w_bf = keep.tile([P, PASSES * M * PACK], BF16, name="w_bf", align_bytes=64)
+        w_codes = keep.tile([P, PASSES * M], U32, name="w_codes", align_bytes=64)
+        w_scale = keep.tile([P, PASSES * M], U8, name="w_scale", align_bytes=64)
+        for o in range(PASSES):
+            nc.scalar.copy(
+                w_bf[:, o * M * PACK : (o + 1) * M * PACK].rearrange("p (m j) -> p m j", j=PACK),
+                w_raw[o][:].rearrange("p j m -> p m j"),
+            )
+
+        x_codes = [
+            [
+                keep.tile([P, HALF], U32, name="x_codes%d%d" % (o, h), align_bytes=64,
+                          tag="scales_then_codes" if (o, h) == (0, 0) else "x_codes%d%d" % (o, h))
+                for h in range(2)
+            ]
+            for o in range(PASSES)
+        ]
+        banks = [psum.tile([P, hi - lo], F32, name="bank%d" % g) for g, (lo, hi) in enumerate(GROUPS)]
+
+        def gather(o, h):
+            nc.vector.tensor_copy(
+                x_codes[o][h][:],
+                word_tables[o][:].bitcast(U32).indirect(offsets[:, h * HALF // 16 : (h + 1) * HALF // 16]),
+            )
+
+        def multiply(o, g):
+            lo, hi = GROUPS[g]
+            h = lo // HALF
+            nc.tensor.matmul_mx(
+                out=banks[g][:],
+                lhsT=w_codes[:, o * M : (o + 1) * M].bitcast(FP8X4),
+                lhsT_scale=w_scale[:, o * M : (o + 1) * M],
+                rhs=x_codes[o][h][:, lo - h * HALF : hi - h * HALF].bitcast(FP8X4),
+                rhs_scale=x_scale[4 * o : P, lo:hi],
+                start=(o == 0),
+                stop=(o == PASSES - 1),
+            )
+
+        gather(0, 0)
+        gather(0, 1)
+        nc.vector.quantize_mx(out=w_codes[:].bitcast(FP8X4), scales=w_scale[:], in_=w_bf[:])
+        for g in range(len(GROUPS)):
+            multiply(0, g)
+        gather(1, 0)
+        multiply(1, 0)
+        gather(1, 1)
+        multiply(1, 1)
+        multiply(1, 2)
+
+        log_truth = keep.tile([P, S], F32, name="log_truth")
+        for h in range(2):
+            nc.scalar.activation(log_truth[:, h * HALF : (h + 1) * HALF], truth_sb[h][:], ACT.Ln)
+
+        part_sums = keep.tile([P, len(GROUPS)], F32, name="part_sums")
+        for g, (lo, hi) in enumerate(GROUPS):
+            nc.vector.scalar_tensor_tensor(
+                ld[:, lo:hi], banks[g][:], 1.0, log_truth[:, lo:hi], ALU.mult, ALU.subtract,
+                accum_out=part_sums[:, g : g + 1],
+            )
+        sums_copy = keep.tile([P, len(GROUPS)], F32, name="sums_copy")
+        total = keep.tile([P, 1], F32, name="total")
+        nc.scalar.activation(sums_copy[:], part_sums[:], ACT.Copy, accum_out=total[:])
+
+        step = keep.tile([P, S], F32, name="step")
+        half_step = keep.tile([P, S], F32, name="half_step")
+        dev = keep.tile([P, S], F32, name="dev")
+        weighted = keep.tile([P, S], F32, name="weighted")
+        result = keep.tile([P, S], F32, name="result")
+        cols = [slice(c * CHUNK, (c + 1) * CHUNK) for c in range(CHUNKS)]
+
+        for c in range(CHUNKS):
+            nc.vector.tensor_tensor(step[:, cols[c]], ld[:, cols[c]], ld[:, c * CHUNK + 1 : (c + 1) * CHUNK + 1], ALU.subtract)
+
+        def weigh(c):
+            nc.scalar.activation(dev[:, cols[c]], ld[:, cols[c]], ACT.Abs, scale=-float(S), bias=total[:])
+            nc.vector.scalar_tensor_tensor(
+                weighted[:, cols[c]], dev[:, cols[c]], 1.0 / S, valid_sb[:, cols[c]], ALU.mult, ALU.mult
+            )
+
+        def finish(c):
+            nc.scalar.activation(half_step[:, cols[c]], step[:, cols[c]], ACT.Abs, scale=0.5)
+            nc.vector.tensor_tensor(result[:, cols[c]], weighted[:, cols[c]], half_step[:, cols[c]], ALU.add)
+            nc.sync.dma_start(out[:, cols[c]], result[:, cols[c]])
+
+        weigh(0)
+        for c in range(1, CHUNKS):
+            weigh(c)
+            finish(c - 1)
+        finish(CHUNKS - 1)

@@ -31,7 +31,6 @@ def tile_picked_yslog_edge_p_kernel(tc, x_words, x_scales, w1, truth, valid, off
         psum = ctx.enter_context(tc.psum_pool(name="psum", bufs=1))
 
         offsets = keep.tile([P, S // 16], U16, name="offsets")
-        nc.sync.dma_start(offsets[:], offs)
 
         scale_table = keep.tile([P, T], U8, name="scale_table", tag="scales_then_codes", align_bytes=64)
         nc.vector.memset(scale_table[:].bitcast(I32), 0)
@@ -55,6 +54,7 @@ def tile_picked_yslog_edge_p_kernel(tc, x_words, x_scales, w1, truth, valid, off
             nc.sync.dma_start(word_tables[o][:], x_words[o].rearrange("p n t -> p (n t)").bitcast(I32))
 
         load_words(0)
+        nc.sync.dma_start(offsets[:], offs)
         for o in range(PASSES):
             nc.sync.dma_start(w_raw[o][:], w1[o * P * PACK : (o + 1) * P * PACK, :].rearrange("(p j) m -> p j m", j=PACK))
         load_words(1)
@@ -63,7 +63,6 @@ def tile_picked_yslog_edge_p_kernel(tc, x_words, x_scales, w1, truth, valid, off
         nc.sync.dma_start(valid_sb[:], valid)
 
         x_scale = keep.tile([P, S], U8, name="x_scale", align_bytes=64)
-        nc.vector.tensor_copy(x_scale[:], scale_table[:].indirect(offsets[:]))
 
         w_bf = keep.tile([P, PASSES * M * PACK], BF16, name="w_bf", align_bytes=64)
         w_codes = keep.tile([P, PASSES * M], U32, name="w_codes", align_bytes=64)
@@ -75,42 +74,36 @@ def tile_picked_yslog_edge_p_kernel(tc, x_words, x_scales, w1, truth, valid, off
             )
 
         x_codes = [
-            [
-                keep.tile([P, HALF], U32, name="x_codes%d%d" % (o, h), align_bytes=64,
-                          tag="scales_then_codes" if (o, h) == (0, 0) else "x_codes%d%d" % (o, h))
-                for h in range(2)
-            ]
-            for o in range(PASSES)
+            keep.tile([P, S], U32, name="x_codes0", align_bytes=64),
+            keep.tile([P, S], U32, name="x_codes1", tag="scales_then_codes", align_bytes=64),
         ]
         banks = [psum.tile([P, hi - lo], F32, name="bank%d" % g) for g, (lo, hi) in enumerate(GROUPS)]
 
-        def gather(o, h):
+        def gather(o, lo, hi):
             nc.vector.tensor_copy(
-                x_codes[o][h][:],
-                word_tables[o][:].bitcast(U32).indirect(offsets[:, h * HALF // 16 : (h + 1) * HALF // 16]),
+                x_codes[o][:, lo:hi], word_tables[o][:].bitcast(U32).indirect(offsets[:, lo // 16 : hi // 16])
             )
 
         def multiply(o, g):
             lo, hi = GROUPS[g]
-            h = lo // HALF
             nc.tensor.matmul_mx(
                 out=banks[g][:],
                 lhsT=w_codes[:, o * M : (o + 1) * M].bitcast(FP8X4),
                 lhsT_scale=w_scale[:, o * M : (o + 1) * M],
-                rhs=x_codes[o][h][:, lo - h * HALF : hi - h * HALF].bitcast(FP8X4),
+                rhs=x_codes[o][:, lo:hi].bitcast(FP8X4),
                 rhs_scale=x_scale[4 * o : P, lo:hi],
                 start=(o == 0),
                 stop=(o == PASSES - 1),
             )
 
-        gather(0, 0)
-        gather(0, 1)
+        gather(0, 0, S)
         nc.vector.quantize_mx(out=w_codes[:].bitcast(FP8X4), scales=w_scale[:], in_=w_bf[:])
+        nc.vector.tensor_copy(x_scale[:], scale_table[:].indirect(offsets[:]))
         for g in range(len(GROUPS)):
             multiply(0, g)
-        gather(1, 0)
+        gather(1, 0, HALF)
         multiply(1, 0)
-        gather(1, 1)
+        gather(1, HALF, S)
         multiply(1, 1)
         multiply(1, 2)
 

@@ -20,8 +20,9 @@ PACK = 4
 PASSES = K // (P * PACK)
 HALF = S // 2
 GROUPS = ((0, 512), (512, 768), (768, 1024))
-CHUNK = 256
-CHUNKS = S // CHUNK
+LEAD = 264
+CHUNKS = ((0, 256), (256, 640), (640, 896), (896, 1024))
+HEAD = 1024
 
 
 def tile_picked_yslog_edge_p_kernel(tc, x_words, x_scales, w1, truth, valid, offs, out):
@@ -31,38 +32,46 @@ def tile_picked_yslog_edge_p_kernel(tc, x_words, x_scales, w1, truth, valid, off
         psum = ctx.enter_context(tc.psum_pool(name="psum", bufs=1))
 
         offsets = keep.tile([P, S // 16], U16, name="offsets")
-
-        scale_table = keep.tile([P, T], U8, name="scale_table", tag="scales_then_codes", align_bytes=64)
+        scale_table = keep.tile([P, T], U8, name="scale_table", align_bytes=64)
         nc.vector.memset(scale_table[:].bitcast(I32), 0)
-        scale_rows = x_scales.bitcast(I32)
-        for q in range(4):
-            nc.gpsimd.dma_start(
-                scale_table[:].bitcast(I32)[32 * q : 32 * q + 4 * PASSES, :], scale_rows[:, 4 * q : 4 * q + 4, :]
-            )
+        x_scale = [keep.tile([P, S], U8, name="x_scale%d" % o, align_bytes=64) for o in range(PASSES)]
+        for o in range(PASSES):
+            nc.vector.memset(x_scale[o][:].bitcast(I32), 0)
 
         ld = keep.tile([P, S + 8], F32, name="ld")
         one = keep.tile([P, 1], F32, name="one")
         nc.vector.memset(one[:], 1.0)
         nc.scalar.activation(ld[:, S : S + 1], one[:], ACT.Ln)
 
-        word_tables = [keep.tile([P, T], I32, name="word_table%d" % o, align_bytes=64) for o in range(PASSES)]
-        w_raw = [keep.tile([P, PACK, M], F32, name="w_raw%d" % o) for o in range(PASSES)]
-        truth_sb = [keep.tile([P, HALF], F32, name="truth%d" % h) for h in range(2)]
-        valid_sb = keep.tile([P, S], F32, name="valid_sb")
+        word_tables = [
+            keep.tile([P, T], I32, name="word_table0", align_bytes=64),
+            keep.tile([P, T], I32, name="word_table1", align_bytes=64),
+        ]
+        w_raw = keep.tile([P, PASSES, PACK * M], F32, name="w_raw")
 
-        def load_words(o):
-            nc.sync.dma_start(word_tables[o][:], x_words[o].rearrange("p n t -> p (n t)").bitcast(I32))
+        def load_words(o, lo, hi):
+            nc.sync.dma_start(word_tables[o][:, lo:hi], x_words[o].rearrange("p n t -> p (n t)").bitcast(I32)[:, lo:hi])
 
-        load_words(0)
+        load_words(0, 0, HEAD)
         nc.sync.dma_start(offsets[:], offs)
-        for o in range(PASSES):
-            nc.sync.dma_start(w_raw[o][:], w1[o * P * PACK : (o + 1) * P * PACK, :].rearrange("(p j) m -> p j m", j=PACK))
-        load_words(1)
-        for h in range(2):
-            nc.sync.dma_start(truth_sb[h][:], truth[:, h * HALF : (h + 1) * HALF])
-        nc.sync.dma_start(valid_sb[:], valid)
+        nc.sync.dma_start(scale_table[:].bitcast(I32)[0:P:4, :], x_scales.rearrange("o r n -> (o r) n").bitcast(I32))
+        load_words(0, HEAD, T)
+        nc.sync.dma_start(w_raw[:], w1.rearrange("(o p j) m -> p o (j m)", o=PASSES, j=PACK))
 
-        x_scale = keep.tile([P, S], U8, name="x_scale", align_bytes=64)
+        picked_scales = keep.tile([P, S], U8, name="picked_scales", align_bytes=64)
+        nc.vector.tensor_copy(picked_scales[:], scale_table[:].indirect(offsets[:]))
+
+        def place_scales(o):
+            for i in range(4):
+                nc.sync.dma_start(
+                    x_scale[o][:].bitcast(I32)[4 * o + i : P : 32, :],
+                    picked_scales[:].bitcast(I32)[64 * o + 4 * i : 64 * (o + 1) : 16, :],
+                )
+
+        load_words(1, 0, T // 2)
+        place_scales(0)
+        load_words(1, T // 2, T)
+        place_scales(1)
 
         w_bf = keep.tile([P, PASSES * M * PACK], BF16, name="w_bf", align_bytes=64)
         w_codes = keep.tile([P, PASSES * M], U32, name="w_codes", align_bytes=64)
@@ -70,13 +79,10 @@ def tile_picked_yslog_edge_p_kernel(tc, x_words, x_scales, w1, truth, valid, off
         for o in range(PASSES):
             nc.scalar.copy(
                 w_bf[:, o * M * PACK : (o + 1) * M * PACK].rearrange("p (m j) -> p m j", j=PACK),
-                w_raw[o][:].rearrange("p j m -> p m j"),
+                w_raw[:, o, :].rearrange("p (j m) -> p m j", j=PACK),
             )
 
-        x_codes = [
-            keep.tile([P, S], U32, name="x_codes0", align_bytes=64),
-            keep.tile([P, S], U32, name="x_codes1", tag="scales_then_codes", align_bytes=64),
-        ]
+        x_codes = [keep.tile([P, S], U32, name="x_codes%d" % o, align_bytes=64) for o in range(PASSES)]
         banks = [psum.tile([P, hi - lo], F32, name="bank%d" % g) for g, (lo, hi) in enumerate(GROUPS)]
 
         def gather(o, lo, hi):
@@ -91,59 +97,79 @@ def tile_picked_yslog_edge_p_kernel(tc, x_words, x_scales, w1, truth, valid, off
                 lhsT=w_codes[:, o * M : (o + 1) * M].bitcast(FP8X4),
                 lhsT_scale=w_scale[:, o * M : (o + 1) * M],
                 rhs=x_codes[o][:, lo:hi].bitcast(FP8X4),
-                rhs_scale=x_scale[4 * o : P, lo:hi],
+                rhs_scale=x_scale[o][4 * o : P, lo:hi],
                 start=(o == 0),
                 stop=(o == PASSES - 1),
             )
 
         gather(0, 0, S)
         nc.vector.quantize_mx(out=w_codes[:].bitcast(FP8X4), scales=w_scale[:], in_=w_bf[:])
-        nc.vector.tensor_copy(x_scale[:], scale_table[:].indirect(offsets[:]))
+
+        truth_sb = keep.tile([P, S], F32, name="truth_sb")
+        valid_sb = keep.tile([P, S], F32, name="valid_sb", align_bytes=64)
+        for h in range(2):
+            nc.sync.dma_start(truth_sb[:, h * HALF : (h + 1) * HALF], truth[:, h * HALF : (h + 1) * HALF])
+        nc.sync.dma_start(valid_sb[:], valid)
+
         for g in range(len(GROUPS)):
             multiply(0, g)
         gather(1, 0, HALF)
         multiply(1, 0)
         gather(1, HALF, S)
-        multiply(1, 1)
-        multiply(1, 2)
+        for g in range(1, len(GROUPS)):
+            multiply(1, g)
 
         log_truth = keep.tile([P, S], F32, name="log_truth")
         for h in range(2):
-            nc.scalar.activation(log_truth[:, h * HALF : (h + 1) * HALF], truth_sb[h][:], ACT.Ln)
+            nc.scalar.activation(log_truth[:, h * HALF : (h + 1) * HALF], truth_sb[:, h * HALF : (h + 1) * HALF], ACT.Ln)
 
-        part_sums = keep.tile([P, len(GROUPS)], F32, name="part_sums")
-        for g, (lo, hi) in enumerate(GROUPS):
-            nc.vector.scalar_tensor_tensor(
-                ld[:, lo:hi], banks[g][:], 1.0, log_truth[:, lo:hi], ALU.mult, ALU.subtract,
-                accum_out=part_sums[:, g : g + 1],
-            )
-        sums_copy = keep.tile([P, len(GROUPS)], F32, name="sums_copy")
+        pieces = [(0, 0, LEAD), (0, LEAD, HALF)] + [(g, GROUPS[g][0], GROUPS[g][1]) for g in range(1, len(GROUPS))]
+        part_sums = keep.tile([P, len(pieces)], F32, name="part_sums")
+        sums_copy = keep.tile([P, len(pieces)], F32, name="sums_copy")
         total = keep.tile([P, 1], F32, name="total")
-        nc.scalar.activation(sums_copy[:], part_sums[:], ACT.Copy, accum_out=total[:])
-
         step = keep.tile([P, S], F32, name="step")
         half_step = keep.tile([P, S], F32, name="half_step")
         dev = keep.tile([P, S], F32, name="dev")
         weighted = keep.tile([P, S], F32, name="weighted")
         result = keep.tile([P, S], F32, name="result")
-        cols = [slice(c * CHUNK, (c + 1) * CHUNK) for c in range(CHUNKS)]
 
-        for c in range(CHUNKS):
-            nc.vector.tensor_tensor(step[:, cols[c]], ld[:, cols[c]], ld[:, c * CHUNK + 1 : (c + 1) * CHUNK + 1], ALU.subtract)
-
-        def weigh(c):
-            nc.scalar.activation(dev[:, cols[c]], ld[:, cols[c]], ACT.Abs, scale=-float(S), bias=total[:])
+        def residual(n):
+            g, lo, hi = pieces[n]
+            base = GROUPS[g][0]
             nc.vector.scalar_tensor_tensor(
-                weighted[:, cols[c]], dev[:, cols[c]], 1.0 / S, valid_sb[:, cols[c]], ALU.mult, ALU.mult
+                ld[:, lo:hi], banks[g][:, lo - base : hi - base], 1.0, log_truth[:, lo:hi], ALU.mult, ALU.subtract,
+                accum_out=part_sums[:, n : n + 1],
             )
 
-        def finish(c):
-            nc.scalar.activation(half_step[:, cols[c]], step[:, cols[c]], ACT.Abs, scale=0.5)
-            nc.vector.tensor_tensor(result[:, cols[c]], weighted[:, cols[c]], half_step[:, cols[c]], ALU.add)
-            nc.sync.dma_start(out[:, cols[c]], result[:, cols[c]])
+        def difference(lo, hi):
+            nc.vector.tensor_tensor(step[:, lo:hi], ld[:, lo:hi], ld[:, lo + 1 : hi + 1], ALU.subtract)
 
-        weigh(0)
-        for c in range(1, CHUNKS):
-            weigh(c)
-            finish(c - 1)
-        finish(CHUNKS - 1)
+        def halve(lo, hi):
+            nc.scalar.activation(half_step[:, lo:hi], step[:, lo:hi], ACT.Abs, scale=0.5)
+
+        def weigh(lo, hi):
+            nc.scalar.activation(dev[:, lo:hi], ld[:, lo:hi], ACT.Abs, scale=-float(S), bias=total[:])
+            nc.vector.scalar_tensor_tensor(weighted[:, lo:hi], dev[:, lo:hi], 1.0 / S, valid_sb[:, lo:hi], ALU.mult, ALU.mult)
+
+        def finish(lo, hi):
+            nc.vector.tensor_tensor(result[:, lo:hi], weighted[:, lo:hi], half_step[:, lo:hi], ALU.add)
+            nc.sync.dma_start(out[:, lo:hi], result[:, lo:hi])
+
+        residual(0)
+        residual(1)
+        difference(*CHUNKS[0])
+        halve(*CHUNKS[0])
+        for n in range(2, len(pieces)):
+            residual(n)
+        nc.scalar.activation(sums_copy[:], part_sums[:], ACT.Copy, accum_out=total[:])
+        difference(CHUNKS[1][0], S)
+
+        weigh(*CHUNKS[0])
+        weigh(*CHUNKS[1])
+        finish(*CHUNKS[0])
+        for c in range(2, len(CHUNKS)):
+            weigh(*CHUNKS[c])
+            halve(*CHUNKS[c - 1])
+            finish(*CHUNKS[c - 1])
+        halve(*CHUNKS[-1])
+        finish(*CHUNKS[-1])

@@ -34,9 +34,8 @@ def tile_picked_yslog_edge_p_kernel(tc, x_words, x_scales, w1, truth, valid, off
         offsets = keep.tile([P, S // 16], U16, name="offsets")
         scale_table = keep.tile([P, T], U8, name="scale_table", align_bytes=64)
         nc.vector.memset(scale_table[:].bitcast(I32), 0)
-        x_scale = [keep.tile([P, S], U8, name="x_scale%d" % o, align_bytes=64) for o in range(PASSES)]
-        for o in range(PASSES):
-            nc.vector.memset(x_scale[o][:].bitcast(I32), 0)
+        x_scale = keep.tile([P, S], U8, name="x_scale", align_bytes=64)
+        nc.vector.memset(x_scale[:].bitcast(I32), 0)
 
         ld = keep.tile([P, S + 8], F32, name="ld")
         one = keep.tile([P, 1], F32, name="one")
@@ -64,7 +63,7 @@ def tile_picked_yslog_edge_p_kernel(tc, x_words, x_scales, w1, truth, valid, off
         def place_scales(o):
             for i in range(4):
                 nc.sync.dma_start(
-                    x_scale[o][:].bitcast(I32)[4 * o + i : P : 32, :],
+                    x_scale[:].bitcast(I32)[4 * o + i : P : 32, :],
                     picked_scales[:].bitcast(I32)[64 * o + 4 * i : 64 * (o + 1) : 16, :],
                 )
 
@@ -97,7 +96,7 @@ def tile_picked_yslog_edge_p_kernel(tc, x_words, x_scales, w1, truth, valid, off
                 lhsT=w_codes[:, o * M : (o + 1) * M].bitcast(FP8X4),
                 lhsT_scale=w_scale[:, o * M : (o + 1) * M],
                 rhs=x_codes[o][:, lo:hi].bitcast(FP8X4),
-                rhs_scale=x_scale[o][4 * o : P, lo:hi],
+                rhs_scale=x_scale[4 * o : P, lo:hi],
                 start=(o == 0),
                 stop=(o == PASSES - 1),
             )
@@ -162,7 +161,8 @@ def tile_picked_yslog_edge_p_kernel(tc, x_words, x_scales, w1, truth, valid, off
         for n in range(2, len(pieces)):
             residual(n)
         nc.scalar.activation(sums_copy[:], part_sums[:], ACT.Copy, accum_out=total[:])
-        difference(CHUNKS[1][0], S)
+        difference(CHUNKS[1][0], GROUPS[-1][0] - 8)
+        difference(GROUPS[-1][0] - 8, S)
 
         weigh(*CHUNKS[0])
         weigh(*CHUNKS[1])

@@ -22,7 +22,7 @@ HALF = S // 2
 GROUPS = ((0, 512), (512, 768), (768, 1024))
 LEAD = 264
 CHUNKS = ((0, 256), (256, 640), (640, 896), (896, 1024))
-HEAD = 1024
+HEAD = 2048
 
 
 def tile_picked_yslog_edge_p_kernel(tc, x_words, x_scales, w1, truth, valid, offs, out):

from contextlib import ExitStack

import concourse.mybir as mybir

K, T, S, M = 1024, 4096, 1024, 128
FLOPS = 2 * K * S * M

F32 = mybir.dt.float32
BF16 = mybir.dt.bfloat16
I32 = mybir.dt.int32
U32 = mybir.dt.uint32
U16 = mybir.dt.uint16
U8 = mybir.dt.uint8
FP8X4 = mybir.dt.float8_e4m3fn_x4
ALU = mybir.AluOpType
ACT = mybir.ActivationFunctionType

P = 128
PACK = 4
PASSES = K // (P * PACK)
HALF = S // 2
GROUPS = ((0, 512), (512, 768), (768, 1024))
LEAD = 264
CHUNKS = ((0, 256), (256, 640), (640, 896), (896, 1024))
HEAD = 2048


def tile_picked_yslog_edge_p_kernel(tc, x_words, x_scales, w1, truth, valid, offs, out):
    nc = tc.nc
    with ExitStack() as ctx:
        keep = ctx.enter_context(tc.tile_pool(name="keep", bufs=1))
        psum = ctx.enter_context(tc.psum_pool(name="psum", bufs=1))

        offsets = keep.tile([P, S // 16], U16, name="offsets")
        scale_table = keep.tile([P, T], U8, name="scale_table", align_bytes=64)
        nc.vector.memset(scale_table[:].bitcast(I32), 0)
        x_scale = keep.tile([P, S], U8, name="x_scale", align_bytes=64)
        nc.vector.memset(x_scale[:].bitcast(I32), 0)

        ld = keep.tile([P, S + 8], F32, name="ld")
        one = keep.tile([P, 1], F32, name="one")
        nc.vector.memset(one[:], 1.0)
        nc.scalar.activation(ld[:, S : S + 1], one[:], ACT.Ln)

        word_tables = [
            keep.tile([P, T], I32, name="word_table0", align_bytes=64),
            keep.tile([P, T], I32, name="word_table1", align_bytes=64),
        ]
        w_raw = keep.tile([P, PASSES, PACK * M], F32, name="w_raw")

        def load_words(o, lo, hi):
            nc.sync.dma_start(word_tables[o][:, lo:hi], x_words[o].rearrange("p n t -> p (n t)").bitcast(I32)[:, lo:hi])

        load_words(0, 0, HEAD)
        nc.sync.dma_start(offsets[:], offs)
        nc.sync.dma_start(scale_table[:].bitcast(I32)[0:P:4, :], x_scales.rearrange("o r n -> (o r) n").bitcast(I32))
        load_words(0, HEAD, T)
        nc.sync.dma_start(w_raw[:], w1.rearrange("(o p j) m -> p o (j m)", o=PASSES, j=PACK))

        picked_scales = keep.tile([P, S], U8, name="picked_scales", align_bytes=64)
        nc.vector.tensor_copy(picked_scales[:], scale_table[:].indirect(offsets[:]))

        def place_scales(o):
            for i in range(4):
                nc.sync.dma_start(
                    x_scale[:].bitcast(I32)[4 * o + i : P : 32, :],
                    picked_scales[:].bitcast(I32)[64 * o + 4 * i : 64 * (o + 1) : 16, :],
                )

        load_words(1, 0, T // 2)
        place_scales(0)
        load_words(1, T // 2, T)
        place_scales(1)

        w_bf = keep.tile([P, PASSES * M * PACK], BF16, name="w_bf", align_bytes=64)
        w_codes = keep.tile([P, PASSES * M], U32, name="w_codes", align_bytes=64)
        w_scale = keep.tile([P, PASSES * M], U8, name="w_scale", align_bytes=64)
        for o in range(PASSES):
            nc.scalar.copy(
                w_bf[:, o * M * PACK : (o + 1) * M * PACK].rearrange("p (m j) -> p m j", j=PACK),
                w_raw[:, o, :].rearrange("p (j m) -> p m j", j=PACK),
            )

        x_codes = [keep.tile([P, S], U32, name="x_codes%d" % o, align_bytes=64) for o in range(PASSES)]
        banks = [psum.tile([P, hi - lo], F32, name="bank%d" % g) for g, (lo, hi) in enumerate(GROUPS)]

        def gather(o, lo, hi):
            nc.vector.tensor_copy(
                x_codes[o][:, lo:hi], word_tables[o][:].bitcast(U32).indirect(offsets[:, lo // 16 : hi // 16])
            )

        def multiply(o, g):
            lo, hi = GROUPS[g]
            nc.tensor.matmul_mx(
                out=banks[g][:],
                lhsT=w_codes[:, o * M : (o + 1) * M].bitcast(FP8X4),
                lhsT_scale=w_scale[:, o * M : (o + 1) * M],
                rhs=x_codes[o][:, lo:hi].bitcast(FP8X4),
                rhs_scale=x_scale[4 * o : P, lo:hi],
                start=(o == 0),
                stop=(o == PASSES - 1),
            )

        gather(0, 0, S)
        nc.vector.quantize_mx(out=w_codes[:].bitcast(FP8X4), scales=w_scale[:], in_=w_bf[:])

        truth_sb = keep.tile([P, S], F32, name="truth_sb")
        valid_sb = keep.tile([P, S], F32, name="valid_sb", align_bytes=64)
        for h in range(2):
            nc.sync.dma_start(truth_sb[:, h * HALF : (h + 1) * HALF], truth[:, h * HALF : (h + 1) * HALF])
        nc.sync.dma_start(valid_sb[:], valid)

        for g in range(len(GROUPS)):
            multiply(0, g)
        gather(1, 0, HALF)
        multiply(1, 0)
        gather(1, HALF, S)
        for g in range(1, len(GROUPS)):
            multiply(1, g)

        log_truth = keep.tile([P, S], F32, name="log_truth")
        for h in range(2):
            nc.scalar.activation(log_truth[:, h * HALF : (h + 1) * HALF], truth_sb[:, h * HALF : (h + 1) * HALF], ACT.Ln)

        pieces = [(0, 0, LEAD), (0, LEAD, HALF)] + [(g, GROUPS[g][0], GROUPS[g][1]) for g in range(1, len(GROUPS))]
        part_sums = keep.tile([P, len(pieces)], F32, name="part_sums")
        sums_copy = keep.tile([P, len(pieces)], F32, name="sums_copy")
        total = keep.tile([P, 1], F32, name="total")
        step = keep.tile([P, S], F32, name="step")
        half_step = keep.tile([P, S], F32, name="half_step")
        dev = keep.tile([P, S], F32, name="dev")
        weighted = keep.tile([P, S], F32, name="weighted")
        result = keep.tile([P, S], F32, name="result")

        def residual(n):
            g, lo, hi = pieces[n]
            base = GROUPS[g][0]
            nc.vector.scalar_tensor_tensor(
                ld[:, lo:hi], banks[g][:, lo - base : hi - base], 1.0, log_truth[:, lo:hi], ALU.mult, ALU.subtract,
                accum_out=part_sums[:, n : n + 1],
            )

        def difference(lo, hi):
            nc.vector.tensor_tensor(step[:, lo:hi], ld[:, lo:hi], ld[:, lo + 1 : hi + 1], ALU.subtract)

        def halve(lo, hi):
            nc.scalar.activation(half_step[:, lo:hi], step[:, lo:hi], ACT.Abs, scale=0.5)

        def weigh(lo, hi):
            nc.scalar.activation(dev[:, lo:hi], ld[:, lo:hi], ACT.Abs, scale=-float(S), bias=total[:])
            nc.vector.scalar_tensor_tensor(weighted[:, lo:hi], dev[:, lo:hi], 1.0 / S, valid_sb[:, lo:hi], ALU.mult, ALU.mult)

        def finish(lo, hi):
            nc.vector.tensor_tensor(result[:, lo:hi], weighted[:, lo:hi], half_step[:, lo:hi], ALU.add)
            nc.sync.dma_start(out[:, lo:hi], result[:, lo:hi])

        residual(0)
        residual(1)
        difference(*CHUNKS[0])
        halve(*CHUNKS[0])
        for n in range(2, len(pieces)):
            residual(n)
        nc.scalar.activation(sums_copy[:], part_sums[:], ACT.Copy, accum_out=total[:])
        difference(CHUNKS[1][0], GROUPS[-1][0] - 8)
        difference(GROUPS[-1][0] - 8, S)

        weigh(*CHUNKS[0])
        weigh(*CHUNKS[1])
        finish(*CHUNKS[0])
        for c in range(2, len(CHUNKS)):
            weigh(*CHUNKS[c])
            halve(*CHUNKS[c - 1])
            finish(*CHUNKS[c - 1])
        halve(*CHUNKS[-1])
        finish(*CHUNKS[-1])
